import numpy as np
import ml_dtypes


def mxq(x, axis, fmt="e4m3"):
    dtype, down = {"e4m3": (ml_dtypes.float8_e4m3fn, 7), "e5m2": (ml_dtypes.float8_e5m2, 14)}[fmt]
    v = np.moveaxis(np.asarray(x, np.float32).astype(ml_dtypes.bfloat16).astype(np.float64), axis, -1)
    blocks = v.reshape(v.shape[:-1] + (-1, 32))
    amax = np.abs(blocks).max(-1, keepdims=True)
    byte = np.maximum(np.where(amax > 0, np.frexp(amax)[1] - 1 + 127, 0) - down, 1)
    scale = np.exp2(byte - 127.0)
    codes = (blocks / scale).astype(np.float32).astype(dtype).astype(np.float64)
    return np.moveaxis((codes * scale).reshape(v.shape), -1, axis)


WIDE = False


def mx_kscale(k):
    if not WIDE:
        return np.ones(k)
    levels = np.array([30, -30])
    if k % 512:
        return np.exp2(np.random.permutation(np.resize(levels, k // 32))).repeat(32)
    a = np.empty((k // 512, 16))
    for p in range(k // 512):
        a[p, :8] = np.random.permutation(np.resize(levels, 8))
        for g in range(8):
            far = levels[np.abs(levels - a[p, g]) >= 10]
            a[p, g + 8] = far[np.random.randint(len(far))]
    return np.exp2(a.ravel()).repeat(32)


def f64(x):
    return np.asarray(x).astype(np.float64)


def striped(idx):
    return np.tile(np.asarray(idx).reshape(-1, 16).T, (8, 1)).astype(np.uint16)


def unstriped(offs):
    return offs[:16].T.reshape(-1).astype(np.int64)


E2M1 = np.array([0.0, 0.5, 1.0, 1.5, 2.0, 3.0, 4.0, 6.0, -0.0, -0.5, -1.0, -1.5, -2.0, -3.0, -4.0, -6.0])


def pack_weight(w, fmt):
    k, n = w.shape
    w = f64(np.asarray(w, np.float32).astype(ml_dtypes.bfloat16)).reshape(k // 32, 32, n)
    amax = np.abs(w).max(1)
    if fmt in ("e4m3", "e5m2"):
        byte = np.frexp(amax)[1] - 1 + 127 - (7 if fmt == "e4m3" else 14)
    else:
        mant, ex = np.frexp(amax / 6.0)
        byte = np.where(mant > 0.5, ex, ex - 1) + 127
    byte = np.clip(np.where(amax > 0, byte, 1), 1, 254)
    scaled = (w * np.exp2(127.0 - byte)[:, None, :]).reshape(k, n).astype(np.float32)
    by_word = np.ascontiguousarray(scaled.reshape(k // 512, 128, 4, n).transpose(0, 1, 3, 2))
    if fmt in ("e4m3", "e5m2"):
        words = by_word.astype(ml_dtypes.float8_e4m3fn if fmt == "e4m3" else ml_dtypes.float8_e5m2).view(np.uint8)
    else:
        c = by_word.astype(ml_dtypes.float4_e2m1fn).view(np.uint8) & 0xF
        words = (c[..., 0::2] | (c[..., 1::2] << 4)).reshape(k // 512, 128, 2 * n)
    return np.ascontiguousarray(words), np.ascontiguousarray(byte.astype(np.uint8).reshape(k // 512, 16, n))


def unpack_weight(words, scales, fmt):
    g, _, n = scales.shape
    words = np.ascontiguousarray(words).reshape(g, 128, n, -1)
    if fmt in ("e4m3", "e5m2"):
        vals = words.view(ml_dtypes.float8_e4m3fn if fmt == "e4m3" else ml_dtypes.float8_e5m2).astype(np.float64)
    else:
        nib = np.empty((g, 128, n, 4), np.uint8)
        nib[..., 0::2] = words & 0xF
        nib[..., 1::2] = words >> 4
        vals = E2M1[nib]
    vals = vals * np.repeat(np.exp2(scales.astype(np.float64) - 127.0), 8, axis=1)[..., None]
    return vals.transpose(0, 1, 3, 2).reshape(g * 512, n)


K, T, J, N, L = 1024, 1024, 256, 256, 512


def setup_inputs():
    n = np.random.standard_normal
    idx = np.random.permutation(T)[:J]
    fk = mx_kscale(K)
    fl = mx_kscale(L)
    xtp = pack_weight(n((K, T)) * np.random.uniform(0.4, 1.6, (1, T)) / fk[:, None], "e5m2")
    wap = pack_weight(n((K, N)) * 1 / np.sqrt(K) * fk[:, None], "e4m3")
    wbp = pack_weight(n((L, N)) * 1 / np.sqrt(L) * fl[:, None], "e2m1")
    return {
        "xt_words": xtp[0],
        "xt_scales": xtp[1],
        "wa_words": wap[0],
        "wa_scales": wap[1],
        "sx": (n((L, J)) * np.random.uniform(0.4, 1.6, (1, J)) / fl[:, None]).astype(np.float32),
        "wb_words": wbp[0],
        "wb_scales": wbp[1],
        "bi": (np.random.uniform(-0.6, 0.6, (1, N))).astype(np.float32),
        "rs": (1.0 * n((J, N))).astype(np.float32),
        "offs": striped(idx),
    }


def reference(xt_words, xt_scales, wa_words, wa_scales, sx, wb_words, wb_scales, bi, rs, offs):
    idx = unstriped(offs)
    xtu = unpack_weight(xt_words, xt_scales, "e5m2")
    wau = unpack_weight(wa_words, wa_scales, "e4m3")
    wbu = unpack_weight(wb_words, wb_scales, "e2m1")
    xtidxg = xtu[:, idx]
    a = xtidxg.T @ wau
    sxq = mxq(f64(sx), 0, "e5m2")
    b0 = sxq.T @ wbu
    b2 = b0 + f64(bi)
    d = a - b2
    y = d / (np.max(np.abs(d), axis=1, keepdims=True) + 0.2) + 0.3 * f64(rs)
    return y

@@ -1,0 +1,157 @@
+from contextlib import ExitStack
+
+import concourse.mybir as mybir
+from concourse.masks import make_identity
+
+K, T, J, N, L = 1024, 1024, 256, 256, 512
+FLOPS = 2 * J * N * (K + L)
+
+F32 = mybir.dt.float32
+BF16 = mybir.dt.bfloat16
+I32 = mybir.dt.int32
+U32 = mybir.dt.uint32
+U16 = mybir.dt.uint16
+U8 = mybir.dt.uint8
+E4M3X4 = mybir.dt.float8_e4m3fn_x4
+E5M2X4 = mybir.dt.float8_e5m2_x4
+E2M1X4 = mybir.dt.float4_e2m1fn_x4
+ALU = mybir.AluOpType
+COPY = mybir.ActivationFunctionType.Copy
+
+P = 128
+PACK = 4
+PASSES = K // (P * PACK)
+HALVES = J // P
+LIST_COLS = J // 16
+
+
+def tile_list_rows_owninput_gapoverpeak_kernel(
+    tc, xt_words, xt_scales, wa_words, wa_scales, sx, wb_words, wb_scales, bi, rs, offs, out
+):
+    nc = tc.nc
+    with ExitStack() as ctx:
+        sb = ctx.enter_context(tc.tile_pool(name="sb", bufs=1))
+        ps = ctx.enter_context(tc.psum_pool(name="ps", bufs=1))
+
+        offsets = sb.tile([P, LIST_COLS], U16, name="offsets")
+        xt_w = [sb.tile([P, T], U32, name="xt_w%d" % z, align_bytes=64) for z in range(PASSES)]
+        xt_s = sb.tile([P, PASSES, T], U8, name="xt_s", align_bytes=64)
+        wa_w = sb.tile([P, PASSES, N], U32, name="wa_w", align_bytes=64)
+        wb_w = sb.tile([P, 2 * N], U8, name="wb_w", align_bytes=64)
+        wa_s = sb.tile([P, PASSES, N], U8, name="wa_s", align_bytes=64)
+        wb_s = sb.tile([P, 1, N], U8, name="wb_s", align_bytes=64)
+        sx_raw = sb.tile([P, PACK, J], F32, name="sx_raw")
+        bi_col = sb.tile([P, 2], F32, name="bi_col")
+        rs_raw = sb.tile([P, HALVES, N], F32, name="rs_raw")
+        ident = sb.tile([P, P], F32, name="ident")
+
+        nc.vector.memset(xt_s[:].rearrange("p z t -> p (z t)").bitcast(I32), 0)
+        nc.vector.memset(wa_s[:].rearrange("p z n -> p (z n)").bitcast(I32), 0)
+        nc.gpsimd.memset(wb_s[:].rearrange("p z n -> p (z n)").bitcast(I32), 0)
+
+        xt_s_rows = xt_scales.rearrange("z (q r) t -> r q z t", r=4)
+        wa_s_rows = wa_scales.rearrange("z (q r) n -> r q z n", r=4)
+        wb_s_rows = wb_scales.rearrange("z (q r) n -> r q z n", r=4)
+
+        def load_xt_words(z):
+            nc.sync.dma_start(xt_w[z][:].bitcast(I32), xt_words[z].rearrange("p t r -> p (t r)").bitcast(I32))
+
+        nc.sync.dma_start(offsets[:], offs)
+        nc.sync.dma_start(bi_col[:], bi.rearrange("o (p m) -> p (o m)", m=2))
+        nc.sync.dma_start(wb_w[:].bitcast(I32), wb_words[0].bitcast(I32))
+        nc.sync.dma_start(sx_raw[:], sx.rearrange("(p t) j -> p t j", t=PACK))
+        for r in range(4):
+            nc.sync.dma_start(xt_s[r:P:32, :, :].bitcast(I32), xt_s_rows[r].bitcast(I32))
+        for r in range(4):
+            nc.gpsimd.dma_start(wb_s[r:P:32, :, :].bitcast(I32), wb_s_rows[r].bitcast(I32))
+        load_xt_words(0)
+        nc.sync.dma_start(wa_w[:].bitcast(I32), wa_words.rearrange("z p n r -> p z (n r)").bitcast(I32))
+        for r in range(4):
+            nc.sync.dma_start(wa_s[r:P:32, :, :].bitcast(I32), wa_s_rows[r].bitcast(I32))
+        load_xt_words(1)
+        nc.sync.dma_start(rs_raw[:], rs.rearrange("(m p) n -> p m n", p=P))
+
+        make_identity(nc, ident[:])
+
+        bias_ps = ps.tile([P, 2, P], F32, name="bias_ps")
+        for m in range(2):
+            nc.tensor.transpose(bias_ps[:, m, :], bi_col[:, m : m + 1].to_broadcast([P, P]), ident[:])
+        bias = sb.tile([P, P, 2], F32, name="bias")
+
+        g_s = [sb.tile([P, J], U8, name="g_s%d" % z, align_bytes=64) for z in range(PASSES)]
+        for z in range(PASSES):
+            nc.vector.tensor_copy(g_s[z][:], xt_s[:, z, :].indirect(offsets[:]))
+
+        sx_bf = sb.tile([P, J, PACK], BF16, name="sx_bf", align_bytes=64)
+        nc.scalar.activation(
+            sx_bf[:].rearrange("p (c i) t -> p c t i", i=4),
+            sx_raw[:].rearrange("p t (c i) -> p c t i", i=4),
+            COPY,
+            scale=-1.0,
+        )
+        nc.scalar.copy(bias[:], bias_ps[:].rearrange("p m c -> p c m"))
+        sx_w = sb.tile([P, J], U32, name="sx_w", align_bytes=64)
+        sx_s = sb.tile([P, J], U8, name="sx_s", align_bytes=64)
+        g_w0 = sb.tile([P, J], U32, name="g_w0", align_bytes=64)
+        nc.vector.quantize_mx(
+            out=sx_w[:].bitcast(E5M2X4), scales=sx_s[:], in_=sx_bf[:].rearrange("p j t -> p (j t)")
+        )
+        nc.vector.tensor_copy(g_w0[:], xt_w[0][:].indirect(offsets[:]))
+
+        rs3 = sb.tile([P, HALVES, N], F32, name="rs3")
+        nc.scalar.activation(rs3[:], rs_raw[:], COPY, scale=0.3)
+
+        acc = [ps.tile([P, N], F32, name="acc%d" % m) for m in range(HALVES)]
+        for m in range(HALVES):
+            cols = slice(m * P, (m + 1) * P)
+            nc.tensor.matmul_mx(
+                out=acc[m][:],
+                lhsT=g_w0[:, cols].bitcast(E5M2X4),
+                lhsT_scale=g_s[0][:, cols],
+                rhs=wa_w[:, 0, :].bitcast(E4M3X4),
+                rhs_scale=wa_s[:, 0, :],
+                start=True,
+                stop=False,
+            )
+        for m in range(HALVES):
+            cols = slice(m * P, (m + 1) * P)
+            nc.tensor.matmul_mx(
+                out=acc[m][:],
+                lhsT=sx_w[:, cols].bitcast(E5M2X4),
+                lhsT_scale=sx_s[:, cols],
+                rhs=wb_w[:].bitcast(E2M1X4),
+                rhs_scale=wb_s[:, 0, :],
+                start=False,
+                stop=False,
+            )
+        half_cols = LIST_COLS // HALVES
+        for m in range(HALVES):
+            cols = slice(m * P, (m + 1) * P)
+            g_w1 = sb.tile([P, P], U32, name="g_w1_%d" % m, align_bytes=64)
+            nc.vector.tensor_copy(g_w1[:], xt_w[1][:].indirect(offsets[:, m * half_cols : (m + 1) * half_cols]))
+            nc.tensor.matmul_mx(
+                out=acc[m][:],
+                lhsT=g_w1[:].bitcast(E5M2X4),
+                lhsT_scale=g_s[1][:, cols],
+                rhs=wa_w[:, 1, :].bitcast(E4M3X4),
+                rhs_scale=wa_s[:, 1, :],
+                start=False,
+                stop=True,
+            )
+
+        gap = [sb.tile([P, N], F32, name="gap%d" % m) for m in range(HALVES)]
+        peak = [sb.tile([P, 1], F32, name="peak%d" % m) for m in range(HALVES)]
+        den = [sb.tile([P, 1], F32, name="den%d" % m) for m in range(HALVES)]
+        inv = [sb.tile([P, 1], F32, name="inv%d" % m) for m in range(HALVES)]
+        res = [sb.tile([P, N], F32, name="res%d" % m) for m in range(HALVES)]
+        for m in range(HALVES):
+            nc.vector.tensor_tensor(gap[m][:], acc[m][:], bias[:].rearrange("p c m -> p (c m)"), ALU.subtract)
+        for m in range(HALVES):
+            nc.vector.tensor_reduce(peak[m][:], gap[m][:], mybir.AxisListType.X, ALU.max, apply_absolute_value=True)
+        for m in range(HALVES):
+            nc.vector.tensor_scalar(den[m][:], peak[m][:], 0.2, None, ALU.add)
+        for m in range(HALVES):
+            nc.vector.reciprocal(inv[m][:], den[m][:])
+        for m, queue in zip(range(HALVES), (nc.sync, nc.scalar)):
+            nc.vector.scalar_tensor_tensor(res[m][:], gap[m][:], inv[m][:], rs3[:, m, :], ALU.mult, ALU.add)
+            queue.dma_start(out[m * P : (m + 1) * P, :], res[m][:])

@@ -35,41 +35,41 @@ def tile_list_rows_owninput_gapoverpeak_kernel(
 
         offsets = sb.tile([P, LIST_COLS], U16, name="offsets")
         xt_w = [sb.tile([P, T], U32, name="xt_w%d" % z, align_bytes=64) for z in range(PASSES)]
-        xt_s = sb.tile([P, PASSES, T], U8, name="xt_s", align_bytes=64)
-        wa_w = sb.tile([P, PASSES, N], U32, name="wa_w", align_bytes=64)
+        xt_s = sb.tile([P, T], U8, name="xt_s", align_bytes=64)
+        g_s = sb.tile([P, J], U8, name="g_s", tag="g_s_then_wa", align_bytes=64)
+        stage = sb.tile([P, 3 * N], U8, name="stage", align_bytes=64)
+        planes = sb.tile([P, PASSES, 3 * N], U8, name="planes", align_bytes=64)
         wb_w = sb.tile([P, 2 * N], U8, name="wb_w", align_bytes=64)
-        wa_s = sb.tile([P, PASSES, N], U8, name="wa_s", align_bytes=64)
-        wb_s = sb.tile([P, 1, N], U8, name="wb_s", align_bytes=64)
-        sx_raw = sb.tile([P, PACK, J], F32, name="sx_raw")
+        sx_raw = sb.tile([P, PACK, J], F32, name="sx_raw", tag="sx_then_rs")
         bi_col = sb.tile([P, 2], F32, name="bi_col")
-        rs_raw = sb.tile([P, HALVES, N], F32, name="rs_raw")
         ident = sb.tile([P, P], F32, name="ident")
 
-        nc.vector.memset(xt_s[:].rearrange("p z t -> p (z t)").bitcast(I32), 0)
-        nc.vector.memset(wa_s[:].rearrange("p z n -> p (z n)").bitcast(I32), 0)
-        nc.gpsimd.memset(wb_s[:].rearrange("p z n -> p (z n)").bitcast(I32), 0)
-
-        xt_s_rows = xt_scales.rearrange("z (q r) t -> r q z t", r=4)
-        wa_s_rows = wa_scales.rearrange("z (q r) n -> r q z n", r=4)
-        wb_s_rows = wb_scales.rearrange("z (q r) n -> r q z n", r=4)
+        nc.gpsimd.memset(stage[0:32, 2 * N :].bitcast(I32), 0)
+        nc.vector.memset(xt_s[32:64, :].bitcast(I32), 0)
+        nc.vector.memset(xt_s[64:P, :].bitcast(I32), 0)
+        nc.vector.memset(planes[:].rearrange("p z n -> p (z n)").bitcast(I32), 0)
 
         def load_xt_words(z):
             nc.sync.dma_start(xt_w[z][:].bitcast(I32), xt_words[z].rearrange("p t r -> p (t r)").bitcast(I32))
 
         nc.sync.dma_start(offsets[:], offs)
+        nc.sync.dma_start(xt_s[0:32, :].bitcast(I32), xt_scales.rearrange("z r t -> r z t").bitcast(I32))
+        nc.sync.dma_start(sx_raw[:], sx.rearrange("(p t) j -> p t j", t=PACK))
+        nc.sync.dma_start(stage[0:32, N : 2 * N].bitcast(I32), wa_scales.rearrange("z r n -> r z n").bitcast(I32))
+        nc.sync.dma_start(stage[0:32:2, 2 * N :].bitcast(I32), wb_scales[0].bitcast(I32))
         nc.sync.dma_start(bi_col[:], bi.rearrange("o (p m) -> p (o m)", m=2))
         nc.sync.dma_start(wb_w[:].bitcast(I32), wb_words[0].bitcast(I32))
-        nc.sync.dma_start(sx_raw[:], sx.rearrange("(p t) j -> p t j", t=PACK))
-        for r in range(4):
-            nc.sync.dma_start(xt_s[r:P:32, :, :].bitcast(I32), xt_s_rows[r].bitcast(I32))
-        for r in range(4):
-            nc.gpsimd.dma_start(wb_s[r:P:32, :, :].bitcast(I32), wb_s_rows[r].bitcast(I32))
         load_xt_words(0)
-        nc.sync.dma_start(wa_w[:].bitcast(I32), wa_words.rearrange("z p n r -> p z (n r)").bitcast(I32))
-        for r in range(4):
-            nc.sync.dma_start(wa_s[r:P:32, :, :].bitcast(I32), wa_s_rows[r].bitcast(I32))
         load_xt_words(1)
-        nc.sync.dma_start(rs_raw[:], rs.rearrange("(m p) n -> p m n", p=P))
+
+        nc.vector.tensor_copy(g_s[:], xt_s[:].indirect(offsets[:]))
+        nc.vector.tensor_copy(stage[0:32, 0:J].bitcast(I32), g_s[0:32, :].bitcast(I32))
+        for q in range(4):
+            nc.sync.dma_start(
+                planes[32 * q : 32 * q + 4, :, :].bitcast(I32), stage[8 * q : 8 * q + 8, :].bitcast(I32)
+            )
+        wa_w = sb.tile([P, PASSES, N], U32, name="wa_w", tag="g_s_then_wa", align_bytes=64)
+        nc.sync.dma_start(wa_w[:].bitcast(I32), wa_words.rearrange("z p n r -> p z (n r)").bitcast(I32))
 
         make_identity(nc, ident[:])
 
@@ -77,10 +77,6 @@ def tile_list_rows_owninput_gapoverpeak_kernel(
         for m in range(2):
             nc.tensor.transpose(bias_ps[:, m, :], bi_col[:, m : m + 1].to_broadcast([P, P]), ident[:])
         bias = sb.tile([P, P, 2], F32, name="bias")
-
-        g_s = [sb.tile([P, J], U8, name="g_s%d" % z, align_bytes=64) for z in range(PASSES)]
-        for z in range(PASSES):
-            nc.vector.tensor_copy(g_s[z][:], xt_s[:, z, :].indirect(offsets[:]))
 
         sx_bf = sb.tile([P, J, PACK], BF16, name="sx_bf", align_bytes=64)
         nc.scalar.activation(
@@ -98,21 +94,16 @@ def tile_list_rows_owninput_gapoverpeak_kernel(
         )
         nc.vector.tensor_copy(g_w0[:], xt_w[0][:].indirect(offsets[:]))
 
+        rs_raw = sb.tile([P, HALVES, N], F32, name="rs_raw", tag="sx_then_rs")
+        nc.sync.dma_start(rs_raw[:], rs.rearrange("(m p) n -> p m n", p=P))
         rs3 = sb.tile([P, HALVES, N], F32, name="rs3")
         nc.scalar.activation(rs3[:], rs_raw[:], COPY, scale=0.3)
 
         acc = [ps.tile([P, N], F32, name="acc%d" % m) for m in range(HALVES)]
+        half_cols = LIST_COLS // HALVES
+        g_w1 = [sb.tile([P, P], U32, name="g_w1_%d" % m, align_bytes=64) for m in range(HALVES)]
         for m in range(HALVES):
-            cols = slice(m * P, (m + 1) * P)
-            nc.tensor.matmul_mx(
-                out=acc[m][:],
-                lhsT=g_w0[:, cols].bitcast(E5M2X4),
-                lhsT_scale=g_s[0][:, cols],
-                rhs=wa_w[:, 0, :].bitcast(E4M3X4),
-                rhs_scale=wa_s[:, 0, :],
-                start=True,
-                stop=False,
-            )
+            nc.vector.tensor_copy(g_w1[m][:], xt_w[1][:].indirect(offsets[:, m * half_cols : (m + 1) * half_cols]))
         for m in range(HALVES):
             cols = slice(m * P, (m + 1) * P)
             nc.tensor.matmul_mx(
@@ -120,21 +111,27 @@ def tile_list_rows_owninput_gapoverpeak_kernel(
                 lhsT=sx_w[:, cols].bitcast(E5M2X4),
                 lhsT_scale=sx_s[:, cols],
                 rhs=wb_w[:].bitcast(E2M1X4),
-                rhs_scale=wb_s[:, 0, :],
+                rhs_scale=planes[:, 0, 2 * N :],
+                start=True,
+                stop=False,
+            )
+        for m in range(HALVES):
+            cols = slice(m * P, (m + 1) * P)
+            nc.tensor.matmul_mx(
+                out=acc[m][:],
+                lhsT=g_w0[:, cols].bitcast(E5M2X4),
+                lhsT_scale=planes[:, 0, cols],
+                rhs=wa_w[:, 0, :].bitcast(E4M3X4),
+                rhs_scale=planes[:, 0, N : 2 * N],
                 start=False,
                 stop=False,
             )
-        half_cols = LIST_COLS // HALVES
-        for m in range(HALVES):
-            cols = slice(m * P, (m + 1) * P)
-            g_w1 = sb.tile([P, P], U32, name="g_w1_%d" % m, align_bytes=64)
-            nc.vector.tensor_copy(g_w1[:], xt_w[1][:].indirect(offsets[:, m * half_cols : (m + 1) * half_cols]))
             nc.tensor.matmul_mx(
                 out=acc[m][:],
-                lhsT=g_w1[:].bitcast(E5M2X4),
-                lhsT_scale=g_s[1][:, cols],
+                lhsT=g_w1[m][:].bitcast(E5M2X4),
+                lhsT_scale=planes[:, 1, cols],
                 rhs=wa_w[:, 1, :].bitcast(E4M3X4),
-                rhs_scale=wa_s[:, 1, :],
+                rhs_scale=planes[:, 1, N : 2 * N],
                 start=False,
                 stop=True,
             )
@@ -144,14 +141,25 @@ def tile_list_rows_owninput_gapoverpeak_kernel(
         den = [sb.tile([P, 1], F32, name="den%d" % m) for m in range(HALVES)]
         inv = [sb.tile([P, 1], F32, name="inv%d" % m) for m in range(HALVES)]
         res = [sb.tile([P, N], F32, name="res%d" % m) for m in range(HALVES)]
-        for m in range(HALVES):
+
+        def subtract_bias(m):
             nc.vector.tensor_tensor(gap[m][:], acc[m][:], bias[:].rearrange("p c m -> p (c m)"), ALU.subtract)
-        for m in range(HALVES):
+
+        def find_peak(m):
             nc.vector.tensor_reduce(peak[m][:], gap[m][:], mybir.AxisListType.X, ALU.max, apply_absolute_value=True)
-        for m in range(HALVES):
+
+        def add_fifth(m):
             nc.vector.tensor_scalar(den[m][:], peak[m][:], 0.2, None, ALU.add)
-        for m in range(HALVES):
+
+        def invert(m):
             nc.vector.reciprocal(inv[m][:], den[m][:])
-        for m, queue in zip(range(HALVES), (nc.sync, nc.scalar)):
+
+        def finish(m, queue):
             nc.vector.scalar_tensor_tensor(res[m][:], gap[m][:], inv[m][:], rs3[:, m, :], ALU.mult, ALU.add)
             queue.dma_start(out[m * P : (m + 1) * P, :], res[m][:])
+
+        for step in (subtract_bias, find_peak, add_fifth, invert):
+            for m in range(HALVES):
+                step(m)
+        finish(0, nc.sync)
+        finish(1, nc.scalar)

@@ -79,20 +79,21 @@ def tile_list_rows_owninput_gapoverpeak_kernel(
         bias = sb.tile([P, P, 2], F32, name="bias")
 
         sx_bf = sb.tile([P, J, PACK], BF16, name="sx_bf", align_bytes=64)
-        nc.scalar.activation(
+        nc.vector.tensor_scalar(
             sx_bf[:].rearrange("p (c i) t -> p c t i", i=4),
             sx_raw[:].rearrange("p t (c i) -> p c t i", i=4),
-            COPY,
-            scale=-1.0,
+            -1.0,
+            None,
+            ALU.mult,
         )
         nc.scalar.copy(bias[:], bias_ps[:].rearrange("p m c -> p c m"))
         sx_w = sb.tile([P, J], U32, name="sx_w", align_bytes=64)
         sx_s = sb.tile([P, J], U8, name="sx_s", align_bytes=64)
         g_w0 = sb.tile([P, J], U32, name="g_w0", align_bytes=64)
+        nc.vector.tensor_copy(g_w0[:], xt_w[0][:].indirect(offsets[:]))
         nc.vector.quantize_mx(
             out=sx_w[:].bitcast(E5M2X4), scales=sx_s[:], in_=sx_bf[:].rearrange("p j t -> p (j t)")
         )
-        nc.vector.tensor_copy(g_w0[:], xt_w[0][:].indirect(offsets[:]))
 
         rs_raw = sb.tile([P, HALVES, N], F32, name="rs_raw", tag="sx_then_rs")
         nc.sync.dma_start(rs_raw[:], rs.rearrange("(m p) n -> p m n", p=P))

@@ -34,13 +34,13 @@ def tile_list_rows_owninput_gapoverpeak_kernel(
         ps = ctx.enter_context(tc.psum_pool(name="ps", bufs=1))
 
         offsets = sb.tile([P, LIST_COLS], U16, name="offsets")
-        xt_w = [sb.tile([P, T], U32, name="xt_w%d" % z, align_bytes=64) for z in range(PASSES)]
+        xt_w = [sb.tile([P, T], U32, name="xt_w0", align_bytes=64)]
         xt_s = sb.tile([P, T], U8, name="xt_s", align_bytes=64)
         g_s = sb.tile([P, J], U8, name="g_s", tag="g_s_then_wa", align_bytes=64)
         stage = sb.tile([P, 3 * N], U8, name="stage", align_bytes=64)
         planes = sb.tile([P, PASSES, 3 * N], U8, name="planes", align_bytes=64)
         wb_w = sb.tile([P, 2 * N], U8, name="wb_w", align_bytes=64)
-        sx_raw = sb.tile([P, PACK, J], F32, name="sx_raw", tag="sx_then_rs")
+        sx_raw = sb.tile([P, PACK, J], F32, name="sx_raw", tag="sx_then_wa", align_bytes=64)
         bi_col = sb.tile([P, 2], F32, name="bi_col")
         ident = sb.tile([P, P], F32, name="ident")
 
@@ -52,6 +52,9 @@ def tile_list_rows_owninput_gapoverpeak_kernel(
         def load_xt_words(z):
             nc.sync.dma_start(xt_w[z][:].bitcast(I32), xt_words[z].rearrange("p t r -> p (t r)").bitcast(I32))
 
+        def load_wa_words(z):
+            nc.sync.dma_start(wa_w[z][:].bitcast(I32), wa_words[z].rearrange("p n r -> p (n r)").bitcast(I32))
+
         nc.sync.dma_start(offsets[:], offs)
         nc.sync.dma_start(xt_s[0:32, :].bitcast(I32), xt_scales.rearrange("z r t -> r z t").bitcast(I32))
         nc.sync.dma_start(sx_raw[:], sx.rearrange("(p t) j -> p t j", t=PACK))
@@ -60,7 +63,8 @@ def tile_list_rows_owninput_gapoverpeak_kernel(
         nc.sync.dma_start(bi_col[:], bi.rearrange("o (p m) -> p (o m)", m=2))
         nc.sync.dma_start(wb_w[:].bitcast(I32), wb_words[0].bitcast(I32))
         load_xt_words(0)
-        load_xt_words(1)
+        wa_w = [sb.tile([P, N], U32, name="wa_w0", align_bytes=64)]
+        load_wa_words(0)
 
         nc.vector.tensor_copy(g_s[:], xt_s[:].indirect(offsets[:]))
         nc.vector.tensor_copy(stage[0:32, 0:J].bitcast(I32), g_s[0:32, :].bitcast(I32))
@@ -68,8 +72,8 @@ def tile_list_rows_owninput_gapoverpeak_kernel(
             nc.sync.dma_start(
                 planes[32 * q : 32 * q + 4, :, :].bitcast(I32), stage[8 * q : 8 * q + 8, :].bitcast(I32)
             )
-        wa_w = sb.tile([P, PASSES, N], U32, name="wa_w", tag="g_s_then_wa", align_bytes=64)
-        nc.sync.dma_start(wa_w[:].bitcast(I32), wa_words.rearrange("z p n r -> p z (n r)").bitcast(I32))
+        xt_w.append(sb.tile([P, T], U32, name="xt_w1", tag="g_s_then_wa", align_bytes=64))
+        load_xt_words(1)
 
         make_identity(nc, ident[:])
 
@@ -78,7 +82,7 @@ def tile_list_rows_owninput_gapoverpeak_kernel(
             nc.tensor.transpose(bias_ps[:, m, :], bi_col[:, m : m + 1].to_broadcast([P, P]), ident[:])
         bias = sb.tile([P, P, 2], F32, name="bias")
 
-        sx_bf = sb.tile([P, J, PACK], BF16, name="sx_bf", align_bytes=64)
+        sx_bf = sb.tile([P, J, PACK], BF16, name="sx_bf", tag="sx_bf_then_rs", align_bytes=64)
         nc.vector.tensor_scalar(
             sx_bf[:].rearrange("p (c i) t -> p c t i", i=4),
             sx_raw[:].rearrange("p t (c i) -> p c t i", i=4),
@@ -86,6 +90,8 @@ def tile_list_rows_owninput_gapoverpeak_kernel(
             None,
             ALU.mult,
         )
+        wa_w.append(sb.tile([P, N], U32, name="wa_w1", tag="sx_then_wa", align_bytes=64))
+        load_wa_words(1)
         nc.scalar.copy(bias[:], bias_ps[:].rearrange("p m c -> p c m"))
         sx_w = sb.tile([P, J], U32, name="sx_w", align_bytes=64)
         sx_s = sb.tile([P, J], U8, name="sx_s", align_bytes=64)
@@ -95,7 +101,7 @@ def tile_list_rows_owninput_gapoverpeak_kernel(
             out=sx_w[:].bitcast(E5M2X4), scales=sx_s[:], in_=sx_bf[:].rearrange("p j t -> p (j t)")
         )
 
-        rs_raw = sb.tile([P, HALVES, N], F32, name="rs_raw", tag="sx_then_rs")
+        rs_raw = sb.tile([P, HALVES, N], F32, name="rs_raw", tag="sx_bf_then_rs", align_bytes=64)
         nc.sync.dma_start(rs_raw[:], rs.rearrange("(m p) n -> p m n", p=P))
         rs3 = sb.tile([P, HALVES, N], F32, name="rs3")
         nc.scalar.activation(rs3[:], rs_raw[:], COPY, scale=0.3)
@@ -122,16 +128,18 @@ def tile_list_rows_owninput_gapoverpeak_kernel(
                 out=acc[m][:],
                 lhsT=g_w0[:, cols].bitcast(E5M2X4),
                 lhsT_scale=planes[:, 0, cols],
-                rhs=wa_w[:, 0, :].bitcast(E4M3X4),
+                rhs=wa_w[0][:].bitcast(E4M3X4),
                 rhs_scale=planes[:, 0, N : 2 * N],
                 start=False,
                 stop=False,
             )
+        for m in range(HALVES):
+            cols = slice(m * P, (m + 1) * P)
             nc.tensor.matmul_mx(
                 out=acc[m][:],
                 lhsT=g_w1[m][:].bitcast(E5M2X4),
                 lhsT_scale=planes[:, 1, cols],
-                rhs=wa_w[:, 1, :].bitcast(E4M3X4),
+                rhs=wa_w[1][:].bitcast(E4M3X4),
                 rhs_scale=planes[:, 1, N : 2 * N],
                 start=False,
                 stop=True,

from contextlib import ExitStack

import concourse.mybir as mybir
from concourse.masks import make_identity

K, T, J, N, L = 1024, 1024, 256, 256, 512
FLOPS = 2 * J * N * (K + L)

F32 = mybir.dt.float32
BF16 = mybir.dt.bfloat16
I32 = mybir.dt.int32
U32 = mybir.dt.uint32
U16 = mybir.dt.uint16
U8 = mybir.dt.uint8
E4M3X4 = mybir.dt.float8_e4m3fn_x4
E5M2X4 = mybir.dt.float8_e5m2_x4
E2M1X4 = mybir.dt.float4_e2m1fn_x4
ALU = mybir.AluOpType
COPY = mybir.ActivationFunctionType.Copy

P = 128
PACK = 4
PASSES = K // (P * PACK)
HALVES = J // P
LIST_COLS = J // 16


def tile_list_rows_owninput_gapoverpeak_kernel(
    tc, xt_words, xt_scales, wa_words, wa_scales, sx, wb_words, wb_scales, bi, rs, offs, out
):
    nc = tc.nc
    with ExitStack() as ctx:
        sb = ctx.enter_context(tc.tile_pool(name="sb", bufs=1))
        ps = ctx.enter_context(tc.psum_pool(name="ps", bufs=1))

        offsets = sb.tile([P, LIST_COLS], U16, name="offsets")
        xt_w = [sb.tile([P, T], U32, name="xt_w0", align_bytes=64)]
        xt_s = sb.tile([P, T], U8, name="xt_s", align_bytes=64)
        g_s = sb.tile([P, J], U8, name="g_s", tag="g_s_then_wa", align_bytes=64)
        stage = sb.tile([P, 3 * N], U8, name="stage", align_bytes=64)
        planes = sb.tile([P, PASSES, 3 * N], U8, name="planes", align_bytes=64)
        wb_w = sb.tile([P, 2 * N], U8, name="wb_w", align_bytes=64)
        sx_raw = sb.tile([P, PACK, J], F32, name="sx_raw", tag="sx_then_wa", align_bytes=64)
        bi_col = sb.tile([P, 2], F32, name="bi_col")
        ident = sb.tile([P, P], F32, name="ident")

        nc.gpsimd.memset(stage[0:32, 2 * N :].bitcast(I32), 0)
        nc.vector.memset(xt_s[32:64, :].bitcast(I32), 0)
        nc.vector.memset(xt_s[64:P, :].bitcast(I32), 0)
        nc.vector.memset(planes[:].rearrange("p z n -> p (z n)").bitcast(I32), 0)

        def load_xt_words(z):
            nc.sync.dma_start(xt_w[z][:].bitcast(I32), xt_words[z].rearrange("p t r -> p (t r)").bitcast(I32))

        def load_wa_words(z):
            nc.sync.dma_start(wa_w[z][:].bitcast(I32), wa_words[z].rearrange("p n r -> p (n r)").bitcast(I32))

        nc.sync.dma_start(offsets[:], offs)
        nc.sync.dma_start(xt_s[0:32, :].bitcast(I32), xt_scales.rearrange("z r t -> r z t").bitcast(I32))
        nc.sync.dma_start(sx_raw[:], sx.rearrange("(p t) j -> p t j", t=PACK))
        nc.sync.dma_start(stage[0:32, N : 2 * N].bitcast(I32), wa_scales.rearrange("z r n -> r z n").bitcast(I32))
        nc.sync.dma_start(stage[0:32:2, 2 * N :].bitcast(I32), wb_scales[0].bitcast(I32))
        nc.sync.dma_start(bi_col[:], bi.rearrange("o (p m) -> p (o m)", m=2))
        nc.sync.dma_start(wb_w[:].bitcast(I32), wb_words[0].bitcast(I32))
        load_xt_words(0)
        wa_w = [sb.tile([P, N], U32, name="wa_w0", align_bytes=64)]
        load_wa_words(0)

        nc.vector.tensor_copy(g_s[:], xt_s[:].indirect(offsets[:]))
        nc.vector.tensor_copy(stage[0:32, 0:J].bitcast(I32), g_s[0:32, :].bitcast(I32))
        for q in range(4):
            nc.sync.dma_start(
                planes[32 * q : 32 * q + 4, :, :].bitcast(I32), stage[8 * q : 8 * q + 8, :].bitcast(I32)
            )
        xt_w.append(sb.tile([P, T], U32, name="xt_w1", tag="g_s_then_wa", align_bytes=64))
        load_xt_words(1)

        make_identity(nc, ident[:])

        bias_ps = ps.tile([P, 2, P], F32, name="bias_ps")
        for m in range(2):
            nc.tensor.transpose(bias_ps[:, m, :], bi_col[:, m : m + 1].to_broadcast([P, P]), ident[:])
        bias = sb.tile([P, P, 2], F32, name="bias")

        sx_bf = sb.tile([P, J, PACK], BF16, name="sx_bf", tag="sx_bf_then_rs", align_bytes=64)
        nc.vector.tensor_scalar(
            sx_bf[:].rearrange("p (c i) t -> p c t i", i=4),
            sx_raw[:].rearrange("p t (c i) -> p c t i", i=4),
            -1.0,
            None,
            ALU.mult,
        )
        wa_w.append(sb.tile([P, N], U32, name="wa_w1", tag="sx_then_wa", align_bytes=64))
        load_wa_words(1)
        nc.scalar.copy(bias[:], bias_ps[:].rearrange("p m c -> p c m"))
        sx_w = sb.tile([P, J], U32, name="sx_w", align_bytes=64)
        sx_s = sb.tile([P, J], U8, name="sx_s", align_bytes=64)
        g_w0 = sb.tile([P, J], U32, name="g_w0", align_bytes=64)
        nc.vector.tensor_copy(g_w0[:], xt_w[0][:].indirect(offsets[:]))
        nc.vector.quantize_mx(
            out=sx_w[:].bitcast(E5M2X4), scales=sx_s[:], in_=sx_bf[:].rearrange("p j t -> p (j t)")
        )

        rs_raw = sb.tile([P, HALVES, N], F32, name="rs_raw", tag="sx_bf_then_rs", align_bytes=64)
        nc.sync.dma_start(rs_raw[:], rs.rearrange("(m p) n -> p m n", p=P))
        rs3 = sb.tile([P, HALVES, N], F32, name="rs3")
        nc.scalar.activation(rs3[:], rs_raw[:], COPY, scale=0.3)

        acc = [ps.tile([P, N], F32, name="acc%d" % m) for m in range(HALVES)]
        half_cols = LIST_COLS // HALVES
        g_w1 = [sb.tile([P, P], U32, name="g_w1_%d" % m, align_bytes=64) for m in range(HALVES)]
        for m in range(HALVES):
            nc.vector.tensor_copy(g_w1[m][:], xt_w[1][:].indirect(offsets[:, m * half_cols : (m + 1) * half_cols]))
        for m in range(HALVES):
            cols = slice(m * P, (m + 1) * P)
            nc.tensor.matmul_mx(
                out=acc[m][:],
                lhsT=sx_w[:, cols].bitcast(E5M2X4),
                lhsT_scale=sx_s[:, cols],
                rhs=wb_w[:].bitcast(E2M1X4),
                rhs_scale=planes[:, 0, 2 * N :],
                start=True,
                stop=False,
            )
        for m in range(HALVES):
            cols = slice(m * P, (m + 1) * P)
            nc.tensor.matmul_mx(
                out=acc[m][:],
                lhsT=g_w0[:, cols].bitcast(E5M2X4),
                lhsT_scale=planes[:, 0, cols],
                rhs=wa_w[0][:].bitcast(E4M3X4),
                rhs_scale=planes[:, 0, N : 2 * N],
                start=False,
                stop=False,
            )
        for m in range(HALVES):
            cols = slice(m * P, (m + 1) * P)
            nc.tensor.matmul_mx(
                out=acc[m][:],
                lhsT=g_w1[m][:].bitcast(E5M2X4),
                lhsT_scale=planes[:, 1, cols],
                rhs=wa_w[1][:].bitcast(E4M3X4),
                rhs_scale=planes[:, 1, N : 2 * N],
                start=False,
                stop=True,
            )

        gap = [sb.tile([P, N], F32, name="gap%d" % m) for m in range(HALVES)]
        peak = [sb.tile([P, 1], F32, name="peak%d" % m) for m in range(HALVES)]
        den = [sb.tile([P, 1], F32, name="den%d" % m) for m in range(HALVES)]
        inv = [sb.tile([P, 1], F32, name="inv%d" % m) for m in range(HALVES)]
        res = [sb.tile([P, N], F32, name="res%d" % m) for m in range(HALVES)]

        def subtract_bias(m):
            nc.vector.tensor_tensor(gap[m][:], acc[m][:], bias[:].rearrange("p c m -> p (c m)"), ALU.subtract)

        def find_peak(m):
            nc.vector.tensor_reduce(peak[m][:], gap[m][:], mybir.AxisListType.X, ALU.max, apply_absolute_value=True)

        def add_fifth(m):
            nc.vector.tensor_scalar(den[m][:], peak[m][:], 0.2, None, ALU.add)

        def invert(m):
            nc.vector.reciprocal(inv[m][:], den[m][:])

        def finish(m, queue):
            nc.vector.scalar_tensor_tensor(res[m][:], gap[m][:], inv[m][:], rs3[:, m, :], ALU.mult, ALU.add)
            queue.dma_start(out[m * P : (m + 1) * P, :], res[m][:])

        for step in (subtract_bias, find_peak, add_fifth, invert):
            for m in range(HALVES):
                step(m)
        finish(0, nc.sync)
        finish(1, nc.scalar)
